import numpy as np
import ml_dtypes


def mxq(x, axis, fmt="e4m3"):
    dtype, down = {"e4m3": (ml_dtypes.float8_e4m3fn, 7), "e5m2": (ml_dtypes.float8_e5m2, 14)}[fmt]
    v = np.moveaxis(np.asarray(x, np.float32).astype(ml_dtypes.bfloat16).astype(np.float64), axis, -1)
    blocks = v.reshape(v.shape[:-1] + (-1, 32))
    amax = np.abs(blocks).max(-1, keepdims=True)
    byte = np.maximum(np.where(amax > 0, np.frexp(amax)[1] - 1 + 127, 0) - down, 1)
    scale = np.exp2(byte - 127.0)
    codes = (blocks / scale).astype(np.float32).astype(dtype).astype(np.float64)
    return np.moveaxis((codes * scale).reshape(v.shape), -1, axis)


WIDE = False


def mx_kscale(k):
    if not WIDE:
        return np.ones(k)
    levels = np.array([10, -10, 5, -5, 0])
    if k % 512:
        return np.exp2(np.random.permutation(np.resize(levels, k // 32))).repeat(32)
    a = np.empty((k // 512, 16))
    for p in range(k // 512):
        a[p, :8] = np.random.permutation(np.resize(levels, 8))
        for g in range(8):
            far = levels[np.abs(levels - a[p, g]) >= 10]
            a[p, g + 8] = far[np.random.randint(len(far))]
    return np.exp2(a.ravel()).repeat(32)


BF16 = ml_dtypes.bfloat16


def bf(x):
    return np.asarray(x, np.float32).astype(BF16)


def f64(x):
    return np.asarray(x).astype(np.float64)


E2M1 = np.array([0.0, 0.5, 1.0, 1.5, 2.0, 3.0, 4.0, 6.0, -0.0, -0.5, -1.0, -1.5, -2.0, -3.0, -4.0, -6.0])


def pack_weight(w, fmt):
    k, n = w.shape
    w = f64(bf(w)).reshape(k // 32, 32, n)
    amax = np.abs(w).max(1)
    if fmt == "e4m3":
        byte = np.frexp(amax)[1] - 1 + 127 - 7
    else:
        mant, ex = np.frexp(amax / 6.0)
        byte = np.where(mant > 0.5, ex, ex - 1) + 127
    byte = np.clip(np.where(amax > 0, byte, 1), 1, 254)
    scaled = (w * np.exp2(127.0 - byte)[:, None, :]).reshape(k, n).astype(np.float32)
    by_word = np.ascontiguousarray(scaled.reshape(k // 512, 128, 4, n).transpose(0, 1, 3, 2))
    if fmt == "e4m3":
        words = by_word.astype(ml_dtypes.float8_e4m3fn).view(np.uint8)
    else:
        c = by_word.astype(ml_dtypes.float4_e2m1fn).view(np.uint8) & 0xF
        words = c[..., 0::2] | (c[..., 1::2] << 4)
    return np.ascontiguousarray(words), np.ascontiguousarray(byte.astype(np.uint8).reshape(k // 512, 16, n))


def unpack_weight(words, scales, fmt):
    g, p, n, _ = words.shape
    if fmt == "e4m3":
        vals = np.ascontiguousarray(words).view(ml_dtypes.float8_e4m3fn).astype(np.float64)
    else:
        nib = np.empty((g, p, n, 4), np.uint8)
        nib[..., 0::2] = words & 0xF
        nib[..., 1::2] = words >> 4
        vals = E2M1[nib]
    vals = vals * np.repeat(np.exp2(scales.astype(np.float64) - 127.0), 8, axis=1)[..., None]
    return vals.transpose(0, 1, 3, 2).reshape(g * 512, n)

def planes(Y):
    n, m = Y.shape
    b = f64(bf(Y)).reshape(n // 32, 32, m)
    amax = np.abs(b).max(1)
    byte = np.clip(np.where(amax > 0, np.frexp(amax)[1] - 1 + 127 - 7, 1), 1, 254)
    codes = (b * np.exp2(127.0 - byte)[:, None, :]).reshape(n, m).astype(np.float32).astype(ml_dtypes.float8_e4m3fn).view(np.uint8)
    words = codes.reshape(n // 512, 128, 4, m).transpose(0, 1, 3, 2)
    return np.ascontiguousarray(words), np.ascontiguousarray(byte.astype(np.uint8).reshape(n // 512, 16, m))


B, H, T, S, E = 2, 2, 512, 1024, 512
D = H * E
EPS = 1e-5


def setup_inputs():
    s, t, r = mx_kscale(E), mx_kscale(S), mx_kscale(D)
    q = np.random.standard_normal((B, H, T, E)) * s
    k = np.random.standard_normal((B, H, S, E)) / s
    rab = 0.8 * np.random.standard_normal((H, T, S))
    c = (1.0 + 0.1 * np.random.standard_normal(S)) * t
    v = np.random.standard_normal((B, H, S, E)) + 0.5 * np.random.standard_normal((B, H, S, 1))
    v = v * (0.02 / np.sqrt(S)) / t[:, None]
    x = np.random.standard_normal((B, T, D)) * r
    wu = np.random.standard_normal((D, D)) / np.sqrt(D) / r[:, None]
    wu_words, wu_scales = pack_weight(wu, "e4m3")
    return {"q": bf(q), "k": bf(k), "rab": bf(rab), "c": bf(c), "v": bf(v), "x": bf(x), "wu_words": wu_words, "wu_scales": wu_scales}


def sigmoid(z):
    return 1.0 / (1.0 + np.exp(-z))


def silu_gate(z):
    return z * sigmoid(z)


def plain_layer_norm(p):
    mean = np.mean(p, axis=-1, keepdims=True)
    centered = p - mean
    var = np.mean(centered * centered, axis=-1, keepdims=True)
    return centered / np.sqrt(var + EPS)


def core(q, k, rab, c, v, x, wu_words, wu_scales):
    b, h, t, e = q.shape
    qq = mxq(f64(q), 3, "e4m3")
    kq = mxq(f64(k), 3, "e4m3")
    l = (qq @ kq.transpose(0, 1, 3, 2)) / np.sqrt(e) + f64(rab)[None, :, :, :]
    a = f64(c)[None, None, None, :] * l * sigmoid(l)
    o = mxq(a, 3, "e4m3") @ mxq(f64(v), 2, "e4m3")
    p = np.transpose(o, (0, 2, 1, 3)).reshape(b, t, h * e)
    n = plain_layer_norm(p)
    u = silu_gate(mxq(f64(x), 2, "e4m3") @ unpack_weight(wu_words, wu_scales, "e4m3"))
    return n * u


def reference(q, k, rab, c, v, x, wu_words, wu_scales):
    R_out = core(q, k, rab, c, v, x, wu_words, wu_scales)
    words, scales = planes(np.moveaxis(R_out, 2, 0).reshape(1024, -1))
    return R_out, words, scales

@@ -1,0 +1,306 @@
+from contextlib import ExitStack
+
+import concourse.mybir as mybir
+from concourse.masks import make_identity
+
+B, H, T, S, E = 2, 2, 512, 1024, 512
+D = H * E
+EPS = 1e-5
+FLOPS = 2 * (2 * B * H * T * S * E + B * T * D * D)
+
+F32 = mybir.dt.float32
+BF16 = mybir.dt.bfloat16
+U32 = mybir.dt.uint32
+I32 = mybir.dt.int32
+U8 = mybir.dt.uint8
+FP8X4 = mybir.dt.float8_e4m3fn_x4
+ALU = mybir.AluOpType
+ACT = mybir.ActivationFunctionType
+
+P = 128
+SCALE = 1.0 / float(E) ** 0.5
+
+
+def tile_hstupointwisetransducer_x2_kernel(
+    tc, q, k, rab, c, v, x, wu_words, wu_scales, out_0, out_1, out_2
+):
+    nc = tc.nc
+    with ExitStack() as ctx:
+        const = ctx.enter_context(tc.tile_pool(name="const", bufs=1))
+        rawp = ctx.enter_context(tc.tile_pool(name="rawp", bufs=12))
+        grpp = ctx.enter_context(tc.tile_pool(name="grpp", bufs=4))
+        codep = ctx.enter_context(tc.tile_pool(name="codep", bufs=1))
+        rabp = ctx.enter_context(tc.tile_pool(name="rabp", bufs=4))
+        work = ctx.enter_context(tc.tile_pool(name="work", bufs=3))
+        small = ctx.enter_context(tc.tile_pool(name="small", bufs=4))
+        ps_tr = ctx.enter_context(tc.psum_pool(name="ps_tr", bufs=3))
+        ps_s = ctx.enter_context(tc.psum_pool(name="ps_s", bufs=2))
+        ps_o = ctx.enter_context(tc.psum_pool(name="ps_o", bufs=3))
+
+        ident = const.tile([P, P], F32, name="ident")
+        make_identity(nc, ident[:])
+        neg_half = const.tile([P, 1], F32, name="neg_half")
+        nc.gpsimd.memset(neg_half[:], -0.5)
+        wu_sc = const.tile([P, 2, D], U8, name="wu_sc", align_bytes=64)
+        nc.gpsimd.memset(wu_sc[:].rearrange("p g n -> p (g n)").bitcast(U32), 0)
+
+        c_sb = const.tile([P, 2, 4], BF16, name="c_sb")
+        nc.scalar.dma_start(out=c_sb[:], in_=c.rearrange("(g p t) -> p g t", g=2, t=4))
+
+        def load_raw(src, name):
+            raw = rawp.tile([P, 4, 512], BF16, name=name, tag="raw", align_bytes=64)
+            nc.sync.dma_start(out=raw[:], in_=src)
+            return raw
+
+        def load_q(b, h):
+            return load_raw(q[b, h].rearrange("(a r) e -> r a e", r=P), f"q{b}{h}")
+
+        def load_k(b, h, g):
+            return load_raw(k[b, h, 512 * g : 512 * g + 512].rearrange("(m t) e -> m t e", t=4), f"k{b}{h}{g}")
+
+        def load_v(b, h, g):
+            return load_raw(v[b, h, 512 * g : 512 * g + 512].rearrange("(p t) e -> p t e", t=4), f"v{b}{h}{g}")
+
+        def load_pair(src, name):
+            raw = rawp.tile([P, 2, 1024], BF16, name=name, tag="raw", align_bytes=64)
+            nc.sync.dma_start(out=raw[:], in_=src.rearrange("(a r) s -> r a s", r=P))
+            return raw
+
+        def load_rab(h, half):
+            return load_pair(rab[h, 256 * half : 256 * half + 256], f"rab{h}{half}")
+
+        def load_x(b, half):
+            return load_pair(x[b, 256 * half : 256 * half + 256], f"x{b}{half}")
+
+        raws = {}
+
+        def load(kind, *key):
+            fn = {"q": load_q, "k": load_k, "v": load_v, "r": load_rab, "x": load_x}[kind]
+            raws[(kind,) + key] = fn(*key)
+
+        wu_sb = const.tile([P, 2, D], U32, name="wu_sb", align_bytes=64)
+
+        def load_wu():
+            nc.sync.dma_start(
+                out=wu_sb[:].bitcast(I32),
+                in_=wu_words.rearrange("g p n t -> g p (n t)").bitcast(I32).rearrange("g p n -> p g n"),
+            )
+            for quad in range(4):
+                nc.sync.dma_start(
+                    out=wu_sc[32 * quad : 32 * quad + 4].bitcast(I32),
+                    in_=wu_scales.bitcast(I32)[:, 4 * quad : 4 * quad + 4].rearrange("g r n -> r g n"),
+                )
+
+        for key in (
+            "q00 k000 r00 k001 r01 q01 v000 k010 v001 k011 r10 x00 wu r11 v010 v011 x01 "
+            "q10 k100 k101 v100 q11 v101 k110 k111 x10 v110 v111 x11"
+        ).split():
+            if key == "wu":
+                load_wu()
+            else:
+                load(key[0], *[int(ch) for ch in key[1:]])
+
+        def copy(engine, out, in_):
+            if engine == "V":
+                nc.vector.tensor_copy(out=out, in_=in_)
+            else:
+                nc.scalar.copy(out=out, in_=in_)
+
+        def turn(raw_words, dst_words, engines):
+            for i in range(raw_words.shape[1] // 2):
+                bank = ps_tr.tile([P, 2, 2, P], F32, name="bank", tag="tr")
+                for a in range(2):
+                    for u in range(2):
+                        nc.tensor.transpose(bank[:, a, u, :], raw_words[:, 2 * i + a, u::2], ident[:])
+                copy(engines[i], dst_words[:, 2 * i : 2 * i + 2], bank[:].rearrange("p a u m -> p a m u"))
+
+        def words_of(raw):
+            flat = raw[:].rearrange("p a e -> p (a e)").bitcast(F32)
+            return flat.rearrange("p (a w) -> p a w", w=256)
+
+        def quantized(grp_flat, width, tag, bufs):
+            codes = codep.tile([P, width], U32, name="codes", tag=tag, bufs=bufs, align_bytes=64)
+            scales = codep.tile([P, width], U8, name="scales", tag=tag + "_s", bufs=bufs, align_bytes=64)
+            nc.vector.quantize_mx(out=codes[:].bitcast(FP8X4), scales=scales[:], in_=grp_flat)
+            return codes, scales
+
+        def turned(kind, key, engines, pool, tag):
+            grp = pool.tile([P, 2048], BF16, name="grp", tag=tag, align_bytes=64)
+            dst = grp[:].bitcast(F32).rearrange("p (a m u) -> p a m u", a=4, u=2)
+            turn(words_of(raws[(kind,) + key]), dst, engines)
+            return grp
+
+        ops = {}
+
+        def prep(kind, *key, engines="SS"):
+            grp = turned(kind, key, engines, grpp, "grp")
+            bufs = {"q": 3, "k": 6, "x": 4}[kind]
+            ops[(kind,) + key] = quantized(grp[:], 512, kind + "c", bufs)
+
+        def prep_rab(h, half, engines="SS"):
+            ops["r", h, half] = turned("r", (h, half), engines, rabp, "rabT")
+
+        def prep_v(b, h, g):
+            raw = raws["v", b, h, g]
+            grp = grpp.tile([P, 2048], BF16, name="vgrp", tag="grp", align_bytes=64)
+            for part in range(4):
+                nc.gpsimd.tensor_scalar(
+                    out=grp[:, 512 * part : 512 * part + 512].rearrange("p (e t) -> p e t", t=4),
+                    in0=raw[:, :, 128 * part : 128 * part + 128].rearrange("p t e -> p e t"),
+                    scalar1=1.0,
+                    scalar2=0.0,
+                    op0=ALU.mult,
+                    op1=ALU.add,
+                )
+            ops["v", b, h, g] = quantized(grp[:], 512, "vc", 6)
+
+        def unit(b, h, tb):
+            l = work.tile([P, 1024], F32, name="l", tag="l", bufs=3, align_bytes=64)
+            qc, qs = ops["q", b, h]
+            cols = slice(128 * tb, 128 * tb + 128)
+            rabt = ops["r", h, tb // 2]
+            for g in range(2):
+                kc, ks = ops["k", b, h, g]
+                bank = ps_s.tile([P, 4, P], F32, name="sbank", tag="s")
+                for t in range(4):
+                    kcols = slice(128 * t, 128 * t + 128)
+                    nc.tensor.matmul_mx(
+                        out=bank[:, t, :],
+                        lhsT=kc[:, kcols].bitcast(FP8X4),
+                        lhsT_scale=ks[:, kcols],
+                        rhs=qc[:, cols].bitcast(FP8X4),
+                        rhs_scale=qs[:, cols],
+                        start=True,
+                        stop=True,
+                    )
+                r0 = 1024 * (tb % 2) + 512 * g
+                nc.vector.scalar_tensor_tensor(
+                    out=l[:, 512 * g : 512 * g + 512].rearrange("p (m t) -> p m t", t=4),
+                    in0=bank[:].rearrange("p t m -> p m t"),
+                    scalar=SCALE,
+                    in1=rabt[:, r0 : r0 + 512].rearrange("p (m t) -> p m t", t=4),
+                    op0=ALU.mult,
+                    op1=ALU.add,
+                )
+            nc.scalar.activation(out=l[:], in_=l[:], func=ACT.Silu)
+            a = work.tile([P, 1024], BF16, name="a", tag="a", bufs=3, align_bytes=64)
+            nc.vector.tensor_tensor(
+                out=a[:].rearrange("p (g m t) -> p g m t", g=2, t=4),
+                in0=l[:].rearrange("p (g m t) -> p g m t", g=2, t=4),
+                in1=c_sb[:].unsqueeze(2).to_broadcast([P, 2, P, 4]),
+                op=ALU.mult,
+            )
+            ops["a", b, h, tb] = quantized(a[:], 256, "ac", 12)
+
+        def gate(b, tb):
+            u = work.tile([P, D], F32, name="u", tag="u", bufs=4, align_bytes=64)
+            xc, xs = ops["x", b, tb // 2]
+            for half in range(2):
+                bank = ps_o.tile([P, 512], F32, name="gbank", tag="o")
+                ncols = slice(512 * half, 512 * half + 512)
+                for g in range(2):
+                    x0 = ((tb % 2) * 2 + g) * 128
+                    nc.tensor.matmul_mx(
+                        out=bank[:],
+                        lhsT=xc[:, x0 : x0 + 128].bitcast(FP8X4),
+                        lhsT_scale=xs[:, x0 : x0 + 128],
+                        rhs=wu_sb[:, g, ncols].bitcast(FP8X4),
+                        rhs_scale=wu_sc[:, g, ncols],
+                        start=(g == 0),
+                        stop=(g == 1),
+                    )
+                nc.scalar.activation(out=u[:, ncols], in_=bank[:], func=ACT.Silu)
+            ops["u", b, tb] = u
+
+        def finish(b, tb):
+            u = ops["u", b, tb]
+            stats = small.tile([P, 12], F32, name="stats", tag="stats")
+            banks = []
+            for h in range(H):
+                bank = ps_o.tile([P, 512], F32, name="obank", tag="o")
+                ac, as_ = ops["a", b, h, tb]
+                for g in range(2):
+                    acols = slice(128 * g, 128 * g + 128)
+                    vc, vs = ops["v", b, h, g]
+                    nc.tensor.matmul_mx(
+                        out=bank[:],
+                        lhsT=ac[:, acols].bitcast(FP8X4),
+                        lhsT_scale=as_[:, acols],
+                        rhs=vc[:].bitcast(FP8X4),
+                        rhs_scale=vs[:],
+                        start=(g == 0),
+                        stop=(g == 1),
+                    )
+                nc.vector.bn_stats(out=stats[:, 6 * h : 6 * h + 6], in_=bank[:])
+                banks.append(bank)
+            mv = small.tile([P, 2], F32, name="mv", tag="mv")
+            nc.vector.bn_aggr(out=mv[:], in_=stats[:])
+            ve = small.tile([P, 1], F32, name="ve", tag="ve")
+            nc.gpsimd.tensor_scalar(out=ve[:], in0=mv[:, 1:2], scalar1=EPS, scalar2=None, op0=ALU.add)
+            rstd = small.tile([P, 1], F32, name="rstd", tag="rstd")
+            nc.gpsimd.tensor_tensor(out=rstd[:], in0=ve[:], in1=neg_half[:], op=ALU.pow)
+            y = work.tile([P, D], F32, name="y", tag="y", bufs=3, align_bytes=64)
+            for h in range(H):
+                hc = slice(512 * h, 512 * h + 512)
+                nc.vector.scalar_tensor_tensor(
+                    out=y[:, hc],
+                    in0=banks[h][:],
+                    scalar=mv[:, 0:1],
+                    in1=u[:, hc],
+                    op0=ALU.subtract,
+                    op1=ALU.mult,
+                )
+            yb = work.tile([P, 2, 512], BF16, name="yb", tag="yb", bufs=2, align_bytes=64)
+            nc.scalar.activation(out=yb[:].rearrange("p g d -> p (g d)"), in_=y[:], func=ACT.Copy, scale=rstd[:])
+            nc.scalar.activation(out=y[:], in_=y[:], func=ACT.Copy, scale=rstd[:])
+            nc.sync.dma_start(out=out_0[b, 128 * tb : 128 * tb + 128, :], in_=y[:])
+            ygrp = work.tile([P, 1024], BF16, name="ygrp", tag="ygrp", bufs=2, align_bytes=64)
+            turn(words_of(yb), ygrp[:].bitcast(F32).rearrange("p (a m u) -> p a m u", a=2, u=2), "S")
+            oc, os_ = quantized(ygrp[:], 256, "oc", 2)
+            m0 = 512 * b + 128 * tb
+            nc.sync.dma_start(
+                out=out_1.rearrange("g p m t -> g p (m t)").bitcast(I32)[:, :, m0 : m0 + 128].rearrange("g p m -> p g m"),
+                in_=oc[:].bitcast(I32).rearrange("p (g m) -> p g m", g=2),
+            )
+            for quad in range(4):
+                nc.sync.dma_start(
+                    out=out_2.bitcast(I32)[:, 4 * quad : 4 * quad + 4, m0 // 4 : m0 // 4 + 32].rearrange("g r m -> r g m"),
+                    in_=os_[32 * quad : 32 * quad + 4].bitcast(I32).rearrange("r (g m) -> r g m", g=2),
+                )
+
+        prep("q", 0, 0, engines="SV")
+        prep("k", 0, 0, 0, engines="SV")
+        prep_rab(0, 0, engines="SV")
+        prep("k", 0, 0, 1, engines="SV")
+        plan = {
+            0: "r01 q01 v000",
+            1: "k010 v001",
+            2: "k011 r10",
+            3: "x00 v010",
+            4: "r11 v011 g00 g01",
+            5: "q10 k100 f00",
+            6: "k101 x01 g02 f01",
+            7: "g03 f02",
+            8: "v100 f03",
+            9: "q11 v101",
+            10: "k110 k111",
+            11: "x10 v110",
+            12: "g10 x11 v111",
+            13: "g11 f10",
+            14: "g12 f11",
+            15: "g13 f12 f13",
+        }
+        for step in range(16):
+            unit(step // 8, (step // 4) % 2, step % 4)
+            for item in plan[step].split():
+                kind, key = item[0], [int(ch) for ch in item[1:]]
+                if kind == "r":
+                    prep_rab(*key)
+                elif kind == "v":
+                    prep_v(*key)
+                elif kind == "g":
+                    gate(*key)
+                elif kind == "f":
+                    finish(*key)
+                else:
+                    prep(kind, *key)

@@ -18,7 +18,33 @@ ALU = mybir.AluOpType
 ACT = mybir.ActivationFunctionType
 
 P = 128
+VRAW = 4
 SCALE = 1.0 / float(E) ** 0.5
+
+
+PROGRAM = """
+q00/SV Qq00 k000/SV Qk000 r00/SV k001/SV Qk001 S:0 E:0 S:1 F:0
+E:1 r01/SV S:2 F:1 G:0 q01/SV k010 v0000
+E:2 Qq01 Qk010 k011/SV S:3 F:2 D:0 G:1 r10 Qv0000 v0001 v0010/S
+E:3 Qk011 r11 S:4 F:3 D:1 G:2 Qv0001 Qv0010 v0011 v0100/S
+E:4 x00 S:5 F:4 D:2 G:3 Qv0011 Qv0100 v0101 v0110/S
+E:5 Qx00 x01 S:6 F:5 D:3 G:4 q10 Qv0101 Qv0110 v0111
+E:6 Qx01 Qq10 g:0,0 S:7 F:6 D:4 G:5 g:0,1 k100 k101 Qv0111 v1000
+O:0,0 E:7 Qk100 Qk101 B:0,0 g:0,2 S:8 F:7 D:5 G:6 A:0,0 Y:0,0 Qv1000 v1001
+O:0,1 E:8 B:0,1 g:0,3 S:9 Z:0,0 F:8 D:6 G:7 A:0,1 T:0,0 Y:0,1 Qv1001 v1010
+O:0,2 E:9 B:0,2 q11 S:10 Z:0,1 F:9 D:7 G:8 A:0,2 T:0,1 P:0,0 Y:0,2 Qv1010 v1011
+O:0,3 E:10 Qq11 B:0,3 k110 S:11 Z:0,2 F:10 D:8 G:9 A:0,3 T:0,2 k111 P:0,1 Y:0,3 Qv1011 v1100
+E:11 Qk110 Qk111 x10 S:12 Z:0,3 F:11 D:9 G:10 T:0,3 x11 P:0,2 Qv1100 v1101
+E:12 Qx10 Qx11 g:1,0 S:13 F:12 D:10 G:11 g:1,1 P:0,3 Qv1101 v1110
+E:13 g:1,2 S:14 F:13 D:11 G:12 g:1,3 Qv1110 v1111
+E:14 S:15 F:14 D:12 G:13 Qv1111
+O:1,0 E:15 B:1,0 F:15 D:13 G:14 A:1,0 Y:1,0
+O:1,1 B:1,1 Z:1,0 D:14 G:15 A:1,1 T:1,0 Y:1,1 D:15
+O:1,2 B:1,2 Z:1,1 A:1,2 T:1,1 P:1,0 Y:1,2
+O:1,3 B:1,3 Z:1,2 A:1,3 T:1,2 P:1,1 Y:1,3
+Z:1,3 T:1,3 P:1,2
+P:1,3
+"""
 
 
 def tile_hstupointwisetransducer_x2_kernel(
@@ -27,15 +53,15 @@ def tile_hstupointwisetransducer_x2_kernel(
     nc = tc.nc
     with ExitStack() as ctx:
         const = ctx.enter_context(tc.tile_pool(name="const", bufs=1))
-        rawp = ctx.enter_context(tc.tile_pool(name="rawp", bufs=12))
-        grpp = ctx.enter_context(tc.tile_pool(name="grpp", bufs=4))
+        rawp = ctx.enter_context(tc.tile_pool(name="rawp", bufs=9))
+        grpp = ctx.enter_context(tc.tile_pool(name="grpp", bufs=5))
         codep = ctx.enter_context(tc.tile_pool(name="codep", bufs=1))
         rabp = ctx.enter_context(tc.tile_pool(name="rabp", bufs=4))
         work = ctx.enter_context(tc.tile_pool(name="work", bufs=3))
         small = ctx.enter_context(tc.tile_pool(name="small", bufs=4))
-        ps_tr = ctx.enter_context(tc.psum_pool(name="ps_tr", bufs=3))
+        ps_tr = ctx.enter_context(tc.psum_pool(name="ps_tr", bufs=4))
         ps_s = ctx.enter_context(tc.psum_pool(name="ps_s", bufs=2))
-        ps_o = ctx.enter_context(tc.psum_pool(name="ps_o", bufs=3))
+        ps_o = ctx.enter_context(tc.psum_pool(name="ps_o", bufs=2))
 
         ident = const.tile([P, P], F32, name="ident")
         make_identity(nc, ident[:])
@@ -52,6 +78,11 @@ def tile_hstupointwisetransducer_x2_kernel(
             nc.sync.dma_start(out=raw[:], in_=src)
             return raw
 
+        def load_v_raw(src, name):
+            raw = rawp.tile([P, 4, 512], BF16, name=name, tag="vraw", bufs=VRAW, align_bytes=64)
+            nc.sync.dma_start(out=raw[:], in_=src)
+            return raw
+
         def load_q(b, h):
             return load_raw(q[b, h].rearrange("(a r) e -> r a e", r=P), f"q{b}{h}")
 
@@ -59,7 +90,7 @@ def tile_hstupointwisetransducer_x2_kernel(
             return load_raw(k[b, h, 512 * g : 512 * g + 512].rearrange("(m t) e -> m t e", t=4), f"k{b}{h}{g}")
 
         def load_v(b, h, g):
-            return load_raw(v[b, h, 512 * g : 512 * g + 512].rearrange("(p t) e -> p t e", t=4), f"v{b}{h}{g}")
+            return load_v_raw(v[b, h, 512 * g : 512 * g + 512].rearrange("(p t) e -> p t e", t=4), f"v{b}{h}{g}")
 
         def load_pair(src, name):
             raw = rawp.tile([P, 2, 1024], BF16, name=name, tag="raw", align_bytes=64)
@@ -92,8 +123,7 @@ def tile_hstupointwisetransducer_x2_kernel(
                 )
 
         for key in (
-            "q00 k000 r00 k001 r01 q01 v000 k010 v001 k011 r10 x00 wu r11 v010 v011 x01 "
-            "q10 k100 k101 v100 q11 v101 k110 k111 x10 v110 v111 x11"
+            "q00 k000 r00 k001 r01 q01 k010 v000 k011 r10 v001 r11 v010 x00 v011 wu x01 q10 k100 k101 v100 q11 k110 v101 k111 x10 v110 x11 v111"
         ).split():
             if key == "wu":
                 load_wu()
@@ -132,34 +162,54 @@ def tile_hstupointwisetransducer_x2_kernel(
 
         ops = {}
 
+        grps = {}
+
         def prep(kind, *key, engines="SS"):
-            grp = turned(kind, key, engines, grpp, "grp")
-            bufs = {"q": 3, "k": 6, "x": 4}[kind]
-            ops[(kind,) + key] = quantized(grp[:], 512, kind + "c", bufs)
+            grps[(kind,) + key] = turned(kind, key, engines, grpp, "grp")
 
         def prep_rab(h, half, engines="SS"):
             ops["r", h, half] = turned("r", (h, half), engines, rabp, "rabT")
 
-        def prep_v(b, h, g):
+        def prep_v(b, h, g, half, engine="G"):
             raw = raws["v", b, h, g]
-            grp = grpp.tile([P, 2048], BF16, name="vgrp", tag="grp", align_bytes=64)
-            for part in range(4):
-                nc.gpsimd.tensor_scalar(
-                    out=grp[:, 512 * part : 512 * part + 512].rearrange("p (e t) -> p e t", t=4),
-                    in0=raw[:, :, 128 * part : 128 * part + 128].rearrange("p t e -> p e t"),
-                    scalar1=1.0,
-                    scalar2=0.0,
-                    op0=ALU.mult,
-                    op1=ALU.add,
+            if ("v", b, h, g) not in ops:
+                ops["v", b, h, g] = (
+                    codep.tile([P, 512], U32, name="vcodes", tag="vc", bufs=7, align_bytes=64),
+                    codep.tile([P, 512], U8, name="vscales", tag="vc_s", bufs=7, align_bytes=64),
                 )
-            ops["v", b, h, g] = quantized(grp[:], 512, "vc", 6)
+            grp = grpp.tile([P, 1024], BF16, name="vgrp", tag="vgrp" + engine, bufs=1, align_bytes=64)
+            out = grp[:].rearrange("p (e t) -> p e t", t=4)
+            in_ = raw[:, :, 256 * half : 256 * half + 256].rearrange("p t e -> p e t")
+            if engine == "G":
+                for part in range(1):
+                    w = 256 // 1
+                    nc.gpsimd.tensor_scalar(
+                        out=out[:, w * part : w * part + w], in0=in_[:, w * part : w * part + w],
+                        scalar1=1.0, scalar2=0.0, op0=ALU.mult, op1=ALU.add,
+                    )
+            else:
+                copy(engine, out, in_)
+            grps["v", b, h, g, half] = grp
 
-        def unit(b, h, tb):
-            l = work.tile([P, 1024], F32, name="l", tag="l", bufs=3, align_bytes=64)
+        def quantise(key):
+            grp = grps.pop(key)
+            if key[0] == "v":
+                codes, scales = ops[key[:4]]
+                cols = slice(256 * key[4], 256 * key[4] + 256)
+                nc.vector.quantize_mx(out=codes[:, cols].bitcast(FP8X4), scales=scales[:, cols], in_=grp[:])
+            else:
+                bufs = {"q": 3, "k": 6, "x": 4}[key[0]]
+                ops[key] = quantized(grp[:], 512, key[0] + "c", bufs)
+
+        def scores(n):
+            for g in range(2):
+                scores_half(n, g)
+
+        def scores_half(n, g):
+            b, h, tb = n // 8, (n // 4) % 2, n % 4
             qc, qs = ops["q", b, h]
             cols = slice(128 * tb, 128 * tb + 128)
-            rabt = ops["r", h, tb // 2]
-            for g in range(2):
+            for g in (g,):
                 kc, ks = ops["k", b, h, g]
                 bank = ps_s.tile([P, 4, P], F32, name="sbank", tag="s")
                 for t in range(4):
@@ -173,30 +223,52 @@ def tile_hstupointwisetransducer_x2_kernel(
                         start=True,
                         stop=True,
                     )
+                ops["s", n, g] = bank
+
+        def biased(n):
+            for g in range(2):
+                biased_half(n, g)
+
+        def biased_half(n, g):
+            h, tb = (n // 4) % 2, n % 4
+            rabt = ops["r", h, tb // 2]
+            if g == 0:
+                ops["l", n] = work.tile([P, 1024], F32, name="l", tag="l", bufs=3, align_bytes=64)
+            l = ops["l", n]
+            for g in (g,):
                 r0 = 1024 * (tb % 2) + 512 * g
                 nc.vector.scalar_tensor_tensor(
                     out=l[:, 512 * g : 512 * g + 512].rearrange("p (m t) -> p m t", t=4),
-                    in0=bank[:].rearrange("p t m -> p m t"),
+                    in0=ops["s", n, g][:].rearrange("p t m -> p m t"),
                     scalar=SCALE,
                     in1=rabt[:, r0 : r0 + 512].rearrange("p (m t) -> p m t", t=4),
                     op0=ALU.mult,
                     op1=ALU.add,
                 )
+
+        def silu(n):
+            l = ops["l", n]
             nc.scalar.activation(out=l[:], in_=l[:], func=ACT.Silu)
-            a = work.tile([P, 1024], BF16, name="a", tag="a", bufs=3, align_bytes=64)
+
+        def gained(n):
+            l = ops["l", n]
+            a = work.tile([P, 1024], BF16, name="a", tag="a", bufs=2, align_bytes=64)
             nc.vector.tensor_tensor(
                 out=a[:].rearrange("p (g m t) -> p g m t", g=2, t=4),
                 in0=l[:].rearrange("p (g m t) -> p g m t", g=2, t=4),
                 in1=c_sb[:].unsqueeze(2).to_broadcast([P, 2, P, 4]),
                 op=ALU.mult,
             )
-            ops["a", b, h, tb] = quantized(a[:], 256, "ac", 12)
+            ops["a", n] = a
+
+        def quantise_a(n):
+            ops["a", n] = quantized(ops["a", n][:], 256, "ac", 12)
 
         def gate(b, tb):
-            u = work.tile([P, D], F32, name="u", tag="u", bufs=4, align_bytes=64)
+            u = work.tile([P, D], F32, name="u", tag="u", bufs=5, align_bytes=64)
             xc, xs = ops["x", b, tb // 2]
             for half in range(2):
-                bank = ps_o.tile([P, 512], F32, name="gbank", tag="o")
+                bank = ps_tr.tile([P, 512], F32, name="gbank", tag="tr")
                 ncols = slice(512 * half, 512 * half + 512)
                 for g in range(2):
                     x0 = ((tb % 2) * 2 + g) * 128
@@ -212,13 +284,11 @@ def tile_hstupointwisetransducer_x2_kernel(
                 nc.scalar.activation(out=u[:, ncols], in_=bank[:], func=ACT.Silu)
             ops["u", b, tb] = u
 
-        def finish(b, tb):
-            u = ops["u", b, tb]
-            stats = small.tile([P, 12], F32, name="stats", tag="stats")
+        def weighted_sum(b, tb):
             banks = []
             for h in range(H):
                 bank = ps_o.tile([P, 512], F32, name="obank", tag="o")
-                ac, as_ = ops["a", b, h, tb]
+                ac, as_ = ops["a", 8 * b + 4 * h + tb]
                 for g in range(2):
                     acols = slice(128 * g, 128 * g + 128)
                     vc, vs = ops["v", b, h, g]
@@ -231,32 +301,55 @@ def tile_hstupointwisetransducer_x2_kernel(
                         start=(g == 0),
                         stop=(g == 1),
                     )
-                nc.vector.bn_stats(out=stats[:, 6 * h : 6 * h + 6], in_=bank[:])
                 banks.append(bank)
+            ops["o", b, tb] = banks
+
+        def half_stats(b, tb):
+            stats = small.tile([P, 12], F32, name="stats", tag="stats")
+            for h in range(H):
+                nc.vector.bn_stats(out=stats[:, 6 * h : 6 * h + 6], in_=ops["o", b, tb][h][:])
+            ops["st", b, tb] = stats
+
+        def row_stats(b, tb):
             mv = small.tile([P, 2], F32, name="mv", tag="mv")
-            nc.vector.bn_aggr(out=mv[:], in_=stats[:])
+            nc.vector.bn_aggr(out=mv[:], in_=ops["st", b, tb][:])
             ve = small.tile([P, 1], F32, name="ve", tag="ve")
             nc.gpsimd.tensor_scalar(out=ve[:], in0=mv[:, 1:2], scalar1=EPS, scalar2=None, op0=ALU.add)
             rstd = small.tile([P, 1], F32, name="rstd", tag="rstd")
             nc.gpsimd.tensor_tensor(out=rstd[:], in0=ve[:], in1=neg_half[:], op=ALU.pow)
+            ops["mv", b, tb] = mv, rstd
+
+        def gated(b, tb):
+            u, mv = ops["u", b, tb], ops["mv", b, tb][0]
             y = work.tile([P, D], F32, name="y", tag="y", bufs=3, align_bytes=64)
             for h in range(H):
                 hc = slice(512 * h, 512 * h + 512)
                 nc.vector.scalar_tensor_tensor(
                     out=y[:, hc],
-                    in0=banks[h][:],
+                    in0=ops["o", b, tb][h][:],
                     scalar=mv[:, 0:1],
                     in1=u[:, hc],
                     op0=ALU.subtract,
                     op1=ALU.mult,
                 )
+            ops["y", b, tb] = y
+
+        def scaled(b, tb):
+            y, rstd = ops["y", b, tb], ops["mv", b, tb][1]
             yb = work.tile([P, 2, 512], BF16, name="yb", tag="yb", bufs=2, align_bytes=64)
-            nc.scalar.activation(out=yb[:].rearrange("p g d -> p (g d)"), in_=y[:], func=ACT.Copy, scale=rstd[:])
+            for h in range(H):
+                nc.scalar.activation(out=yb[:, h, :], in_=y[:, 512 * h : 512 * h + 512], func=ACT.Copy, scale=rstd[:])
             nc.scalar.activation(out=y[:], in_=y[:], func=ACT.Copy, scale=rstd[:])
             nc.sync.dma_start(out=out_0[b, 128 * tb : 128 * tb + 128, :], in_=y[:])
+            ops["yb", b, tb] = yb
+
+        def turned_result(b, tb):
             ygrp = work.tile([P, 1024], BF16, name="ygrp", tag="ygrp", bufs=2, align_bytes=64)
-            turn(words_of(yb), ygrp[:].bitcast(F32).rearrange("p (a m u) -> p a m u", a=2, u=2), "S")
-            oc, os_ = quantized(ygrp[:], 256, "oc", 2)
+            turn(words_of(ops["yb", b, tb]), ygrp[:].bitcast(F32).rearrange("p (a m u) -> p a m u", a=2, u=2), "S")
+            ops["yg", b, tb] = ygrp
+
+        def planes(b, tb):
+            oc, os_ = quantized(ops["yg", b, tb][:], 256, "oc", 3)
             m0 = 512 * b + 128 * tb
             nc.sync.dma_start(
                 out=out_1.rearrange("g p m t -> g p (m t)").bitcast(I32)[:, :, m0 : m0 + 128].rearrange("g p m -> p g m"),
@@ -268,39 +361,32 @@ def tile_hstupointwisetransducer_x2_kernel(
                     in_=os_[32 * quad : 32 * quad + 4].bitcast(I32).rearrange("r (g m) -> r g m", g=2),
                 )
 
-        prep("q", 0, 0, engines="SV")
-        prep("k", 0, 0, 0, engines="SV")
-        prep_rab(0, 0, engines="SV")
-        prep("k", 0, 0, 1, engines="SV")
-        plan = {
-            0: "r01 q01 v000",
-            1: "k010 v001",
-            2: "k011 r10",
-            3: "x00 v010",
-            4: "r11 v011 g00 g01",
-            5: "q10 k100 f00",
-            6: "k101 x01 g02 f01",
-            7: "g03 f02",
-            8: "v100 f03",
-            9: "q11 v101",
-            10: "k110 k111",
-            11: "x10 v110",
-            12: "g10 x11 v111",
-            13: "g11 f10",
-            14: "g12 f11",
-            15: "g13 f12 f13",
-        }
-        for step in range(16):
-            unit(step // 8, (step // 4) % 2, step % 4)
-            for item in plan[step].split():
-                kind, key = item[0], [int(ch) for ch in item[1:]]
+        def run(word):
+            kind = word[0]
+            if kind in "qkxr":
+                name, engines = word.split("/") if "/" in word else (word, "SS")
+                key = [int(ch) for ch in name[1:]]
                 if kind == "r":
-                    prep_rab(*key)
-                elif kind == "v":
-                    prep_v(*key)
-                elif kind == "g":
-                    gate(*key)
-                elif kind == "f":
-                    finish(*key)
+                    prep_rab(*key, engines=engines)
                 else:
-                    prep(kind, *key)
+                    prep(kind, *key, engines=engines)
+            elif kind == "v":
+                name, engine = word.split("/") if "/" in word else (word, "G")
+                prep_v(*[int(ch) for ch in name[1:]], engine=engine)
+            elif kind == "Q":
+                quantise((word[1],) + tuple(int(ch) for ch in word[2:]))
+            elif kind in "se":
+                n, g = [int(num) for num in word[2:].split(",")]
+                (scores_half if kind == "s" else biased_half)(n, g)
+            else:
+                name, key = word.split(":")
+                key = [int(n) for n in key.split(",")]
+                table = {
+                    "S": scores, "E": biased, "F": silu, "G": gained, "D": quantise_a, "g": gate,
+                    "O": weighted_sum, "B": half_stats, "A": row_stats, "Y": gated, "Z": scaled, "T": turned_result, "P": planes,
+                }
+                table[name](*key)
+
+        with tc.manual_schedule():
+            for word in PROGRAM.split():
+                run(word)

@@ -6,6 +6,7 @@ from concourse.masks import make_identity
 B, H, T, S, E = 2, 2, 512, 1024, 512
 D = H * E
 EPS = 1e-5
+SCALE = 1.0 / float(E) ** 0.5
 FLOPS = 2 * (2 * B * H * T * S * E + B * T * D * D)
 
 F32 = mybir.dt.float32
@@ -18,33 +19,35 @@ ALU = mybir.AluOpType
 ACT = mybir.ActivationFunctionType
 
 P = 128
-VRAW = 4
-SCALE = 1.0 / float(E) ** 0.5
+GROUP = 512
+BLOCKS = T // P
+UNITS = B * H * BLOCKS
 
+LOADS = (
+    "q00 k000 k001 r00 r01 k010 v000 k011 q01 v011 v010 v001 r10 r11 x00 v101 x01 "
+    "q10 k101 k100 k110 wu k111 x11 q11 x10 v100 v110 v111"
+)
 
-PROGRAM = """
-q00/SV Qq00 k000/SV Qk000 r00/SV k001/SV Qk001 S:0 E:0 S:1 F:0
-E:1 r01/SV S:2 F:1 G:0 q01/SV k010 v0000
-E:2 Qq01 Qk010 k011/SV S:3 F:2 D:0 G:1 r10 Qv0000 v0001 v0010/S
-E:3 Qk011 r11 S:4 F:3 D:1 G:2 Qv0001 Qv0010 v0011 v0100/S
-E:4 x00 S:5 F:4 D:2 G:3 Qv0011 Qv0100 v0101 v0110/S
-E:5 Qx00 x01 S:6 F:5 D:3 G:4 q10 Qv0101 Qv0110 v0111
-E:6 Qx01 Qq10 g:0,0 S:7 F:6 D:4 G:5 g:0,1 k100 k101 Qv0111 v1000
-O:0,0 E:7 Qk100 Qk101 B:0,0 g:0,2 S:8 F:7 D:5 G:6 A:0,0 Y:0,0 Qv1000 v1001
-O:0,1 E:8 B:0,1 g:0,3 S:9 Z:0,0 F:8 D:6 G:7 A:0,1 T:0,0 Y:0,1 Qv1001 v1010
-O:0,2 E:9 B:0,2 q11 S:10 Z:0,1 F:9 D:7 G:8 A:0,2 T:0,1 P:0,0 Y:0,2 Qv1010 v1011
-O:0,3 E:10 Qq11 B:0,3 k110 S:11 Z:0,2 F:10 D:8 G:9 A:0,3 T:0,2 k111 P:0,1 Y:0,3 Qv1011 v1100
-E:11 Qk110 Qk111 x10 S:12 Z:0,3 F:11 D:9 G:10 T:0,3 x11 P:0,2 Qv1100 v1101
-E:12 Qx10 Qx11 g:1,0 S:13 F:12 D:10 G:11 g:1,1 P:0,3 Qv1101 v1110
-E:13 g:1,2 S:14 F:13 D:11 G:12 g:1,3 Qv1110 v1111
-E:14 S:15 F:14 D:12 G:13 Qv1111
-O:1,0 E:15 B:1,0 F:15 D:13 G:14 A:1,0 Y:1,0
-O:1,1 B:1,1 Z:1,0 D:14 G:15 A:1,1 T:1,0 Y:1,1 D:15
-O:1,2 B:1,2 Z:1,1 A:1,2 T:1,1 P:1,0 Y:1,2
-O:1,3 B:1,3 Z:1,2 A:1,3 T:1,2 P:1,1 Y:1,3
-Z:1,3 T:1,3 P:1,2
-P:1,3
-"""
+PLAN = {
+    0: ("k010/SV", "r01 v000.1 v000.0/S"),
+    1: ("k011", "q01 v001.1 v010.0/S"),
+    2: ("r10", "v010.1/S"),
+    3: ("x00", "v001.0"),
+    4: ("r11", "x01/SV"),
+    5: ("q10", "k101 k100 v011.1 v011.0/S"),
+    6: ("g01", ""),
+    7: ("g00", "g03 v100.0"),
+    8: ("k111", "q11 v110.0/S v100.1"),
+    9: ("g02", "k110 v110.1/S v101.0"),
+    10: ("x11", "v111.1/S v101.1"),
+    11: ("x10", ""),
+    12: ("", "v111.0/S"),
+    13: ("g11", ""),
+    14: ("g10", ""),
+    15: ("g13", "g12"),
+}
+STEPS = 20
+FIRST_FINISH = (8, 14)
 
 
 def tile_hstupointwisetransducer_x2_kernel(
@@ -53,15 +56,14 @@ def tile_hstupointwisetransducer_x2_kernel(
     nc = tc.nc
     with ExitStack() as ctx:
         const = ctx.enter_context(tc.tile_pool(name="const", bufs=1))
-        rawp = ctx.enter_context(tc.tile_pool(name="rawp", bufs=9))
-        grpp = ctx.enter_context(tc.tile_pool(name="grpp", bufs=5))
-        codep = ctx.enter_context(tc.tile_pool(name="codep", bufs=1))
-        rabp = ctx.enter_context(tc.tile_pool(name="rabp", bufs=4))
+        inputs = ctx.enter_context(tc.tile_pool(name="inputs", bufs=9))
+        ordered = ctx.enter_context(tc.tile_pool(name="ordered", bufs=5))
+        codes_pool = ctx.enter_context(tc.tile_pool(name="codes_pool", bufs=1))
         work = ctx.enter_context(tc.tile_pool(name="work", bufs=3))
-        small = ctx.enter_context(tc.tile_pool(name="small", bufs=4))
-        ps_tr = ctx.enter_context(tc.psum_pool(name="ps_tr", bufs=4))
-        ps_s = ctx.enter_context(tc.psum_pool(name="ps_s", bufs=2))
-        ps_o = ctx.enter_context(tc.psum_pool(name="ps_o", bufs=2))
+        stat = ctx.enter_context(tc.tile_pool(name="stat", bufs=4))
+        turn_banks = ctx.enter_context(tc.psum_pool(name="turn_banks", bufs=4))
+        score_banks = ctx.enter_context(tc.psum_pool(name="score_banks", bufs=2))
+        sum_banks = ctx.enter_context(tc.psum_pool(name="sum_banks", bufs=2))
 
         ident = const.tile([P, P], F32, name="ident")
         make_identity(nc, ident[:])
@@ -69,66 +71,44 @@ def tile_hstupointwisetransducer_x2_kernel(
         nc.gpsimd.memset(neg_half[:], -0.5)
         wu_sc = const.tile([P, 2, D], U8, name="wu_sc", align_bytes=64)
         nc.gpsimd.memset(wu_sc[:].rearrange("p g n -> p (g n)").bitcast(U32), 0)
+        wu_codes = const.tile([P, 2, D], U32, name="wu_codes", align_bytes=64)
+        gain = const.tile([P, 2, 4], BF16, name="gain")
+        nc.scalar.dma_start(out=gain[:], in_=c.rearrange("(g p t) -> p g t", g=2, t=4))
 
-        c_sb = const.tile([P, 2, 4], BF16, name="c_sb")
-        nc.scalar.dma_start(out=c_sb[:], in_=c.rearrange("(g p t) -> p g t", g=2, t=4))
+        raw = {}
+        ready = {}
+        coded = {}
+        live = {}
 
-        def load_raw(src, name):
-            raw = rawp.tile([P, 4, 512], BF16, name=name, tag="raw", align_bytes=64)
-            nc.sync.dma_start(out=raw[:], in_=src)
-            return raw
-
-        def load_v_raw(src, name):
-            raw = rawp.tile([P, 4, 512], BF16, name=name, tag="vraw", bufs=VRAW, align_bytes=64)
-            nc.sync.dma_start(out=raw[:], in_=src)
-            return raw
-
-        def load_q(b, h):
-            return load_raw(q[b, h].rearrange("(a r) e -> r a e", r=P), f"q{b}{h}")
-
-        def load_k(b, h, g):
-            return load_raw(k[b, h, 512 * g : 512 * g + 512].rearrange("(m t) e -> m t e", t=4), f"k{b}{h}{g}")
-
-        def load_v(b, h, g):
-            return load_v_raw(v[b, h, 512 * g : 512 * g + 512].rearrange("(p t) e -> p t e", t=4), f"v{b}{h}{g}")
-
-        def load_pair(src, name):
-            raw = rawp.tile([P, 2, 1024], BF16, name=name, tag="raw", align_bytes=64)
-            nc.sync.dma_start(out=raw[:], in_=src.rearrange("(a r) s -> r a s", r=P))
-            return raw
-
-        def load_rab(h, half):
-            return load_pair(rab[h, 256 * half : 256 * half + 256], f"rab{h}{half}")
-
-        def load_x(b, half):
-            return load_pair(x[b, 256 * half : 256 * half + 256], f"x{b}{half}")
-
-        raws = {}
-
-        def load(kind, *key):
-            fn = {"q": load_q, "k": load_k, "v": load_v, "r": load_rab, "x": load_x}[kind]
-            raws[(kind,) + key] = fn(*key)
-
-        wu_sb = const.tile([P, 2, D], U32, name="wu_sb", align_bytes=64)
-
-        def load_wu():
-            nc.sync.dma_start(
-                out=wu_sb[:].bitcast(I32),
-                in_=wu_words.rearrange("g p n t -> g p (n t)").bitcast(I32).rearrange("g p n -> p g n"),
-            )
-            for quad in range(4):
+        def load(name):
+            if name == "wu":
                 nc.sync.dma_start(
-                    out=wu_sc[32 * quad : 32 * quad + 4].bitcast(I32),
-                    in_=wu_scales.bitcast(I32)[:, 4 * quad : 4 * quad + 4].rearrange("g r n -> r g n"),
+                    out=wu_codes[:].bitcast(I32),
+                    in_=wu_words.rearrange("g p n t -> g p (n t)").bitcast(I32).rearrange("g p n -> p g n"),
                 )
-
-        for key in (
-            "q00 k000 r00 k001 r01 q01 k010 v000 k011 r10 v001 r11 v010 x00 v011 wu x01 q10 k100 k101 v100 q11 k110 v101 k111 x10 v110 x11 v111"
-        ).split():
-            if key == "wu":
-                load_wu()
+                for j in range(4):
+                    nc.sync.dma_start(
+                        out=wu_sc[32 * j : 32 * j + 4].bitcast(I32),
+                        in_=wu_scales.bitcast(I32)[:, 4 * j : 4 * j + 4].rearrange("g r n -> r g n"),
+                    )
+                return
+            kind, key = name[0], [int(digit) for digit in name[1:]]
+            if kind == "v":
+                raw[name] = inputs.tile([P, 4, 512], BF16, name=name, tag="v_raw", bufs=4, align_bytes=64)
             else:
-                load(key[0], *[int(ch) for ch in key[1:]])
+                raw[name] = inputs.tile([P, 4, 512], BF16, name=name, tag="raw", align_bytes=64)
+            dst = raw[name][:]
+            if kind == "q":
+                src = q[key[0], key[1]].rearrange("(a r) e -> r a e", r=P)
+            elif kind in "kv":
+                tensor = k if kind == "k" else v
+                rows = slice(GROUP * key[2], GROUP * key[2] + GROUP)
+                src = tensor[key[0], key[1], rows].rearrange("(r t) e -> r t e", t=4)
+            else:
+                tensor = rab if kind == "r" else x
+                src = tensor[key[0], 256 * key[1] : 256 * key[1] + 256].rearrange("(a r) s -> r a s", r=P)
+                dst = dst.rearrange("p (a g) e -> p a (g e)", g=2)
+            nc.sync.dma_start(out=dst, in_=src)
 
         def copy(engine, out, in_):
             if engine == "V":
@@ -136,257 +116,273 @@ def tile_hstupointwisetransducer_x2_kernel(
             else:
                 nc.scalar.copy(out=out, in_=in_)
 
-        def turn(raw_words, dst_words, engines):
-            for i in range(raw_words.shape[1] // 2):
-                bank = ps_tr.tile([P, 2, 2, P], F32, name="bank", tag="tr")
-                for a in range(2):
-                    for u in range(2):
-                        nc.tensor.transpose(bank[:, a, u, :], raw_words[:, 2 * i + a, u::2], ident[:])
-                copy(engines[i], dst_words[:, 2 * i : 2 * i + 2], bank[:].rearrange("p a u m -> p a m u"))
-
-        def words_of(raw):
-            flat = raw[:].rearrange("p a e -> p (a e)").bitcast(F32)
+        def as_words(tile):
+            flat = tile[:].rearrange("p a e -> p (a e)").bitcast(F32)
             return flat.rearrange("p (a w) -> p a w", w=256)
 
-        def quantized(grp_flat, width, tag, bufs):
-            codes = codep.tile([P, width], U32, name="codes", tag=tag, bufs=bufs, align_bytes=64)
-            scales = codep.tile([P, width], U8, name="scales", tag=tag + "_s", bufs=bufs, align_bytes=64)
-            nc.vector.quantize_mx(out=codes[:].bitcast(FP8X4), scales=scales[:], in_=grp_flat)
-            return codes, scales
+        def turn(words, dst, engine):
+            bank = turn_banks.tile([P, 2, 2, P], F32, name="turn_bank", tag="turn")
+            for a in range(2):
+                for e in range(2):
+                    nc.tensor.transpose(bank[:, a, e, :], words[:, a, e::2], ident[:])
+            copy(engine, dst, bank[:].rearrange("p a e m -> p a m e"))
 
-        def turned(kind, key, engines, pool, tag):
-            grp = pool.tile([P, 2048], BF16, name="grp", tag=tag, align_bytes=64)
-            dst = grp[:].bitcast(F32).rearrange("p (a m u) -> p a m u", a=4, u=2)
-            turn(words_of(raws[(kind,) + key]), dst, engines)
-            return grp
+        def turn_input(name, engines):
+            tag, bufs = ("rab_turned", 4) if name[0] == "r" else ("ordered", 5)
+            tile = ordered.tile([P, 2048], BF16, name="turned", tag=tag, bufs=bufs, align_bytes=64)
+            dst = tile[:].bitcast(F32).rearrange("p (a m e) -> p a m e", a=4, e=2)
+            for i in range(2):
+                runs = slice(2 * i, 2 * i + 2)
+                turn(as_words(raw[name])[:, runs], dst[:, runs], engines[i])
+            ready[name] = tile
 
-        ops = {}
-
-        grps = {}
-
-        def prep(kind, *key, engines="SS"):
-            grps[(kind,) + key] = turned(kind, key, engines, grpp, "grp")
-
-        def prep_rab(h, half, engines="SS"):
-            ops["r", h, half] = turned("r", (h, half), engines, rabp, "rabT")
-
-        def prep_v(b, h, g, half, engine="G"):
-            raw = raws["v", b, h, g]
-            if ("v", b, h, g) not in ops:
-                ops["v", b, h, g] = (
-                    codep.tile([P, 512], U32, name="vcodes", tag="vc", bufs=7, align_bytes=64),
-                    codep.tile([P, 512], U8, name="vscales", tag="vc_s", bufs=7, align_bytes=64),
-                )
-            grp = grpp.tile([P, 1024], BF16, name="vgrp", tag="vgrp" + engine, bufs=1, align_bytes=64)
-            out = grp[:].rearrange("p (e t) -> p e t", t=4)
-            in_ = raw[:, :, 256 * half : 256 * half + 256].rearrange("p t e -> p e t")
+        def interleave(name, half, engine):
+            tile = ordered.tile([P, 1024], BF16, name="mixed", tag="mixed_" + engine, bufs=1, align_bytes=64)
+            out = tile[:].rearrange("p (e t) -> p e t", t=4)
+            in_ = raw[name][:, :, 256 * half : 256 * half + 256].rearrange("p t e -> p e t")
             if engine == "G":
-                for part in range(1):
-                    w = 256 // 1
-                    nc.gpsimd.tensor_scalar(
-                        out=out[:, w * part : w * part + w], in0=in_[:, w * part : w * part + w],
-                        scalar1=1.0, scalar2=0.0, op0=ALU.mult, op1=ALU.add,
-                    )
+                nc.gpsimd.tensor_scalar(out=out, in0=in_, scalar1=1.0, scalar2=0.0, op0=ALU.mult, op1=ALU.add)
             else:
                 copy(engine, out, in_)
-            grps["v", b, h, g, half] = grp
+            ready[name, half] = tile
 
-        def quantise(key):
-            grp = grps.pop(key)
-            if key[0] == "v":
-                codes, scales = ops[key[:4]]
-                cols = slice(256 * key[4], 256 * key[4] + 256)
-                nc.vector.quantize_mx(out=codes[:, cols].bitcast(FP8X4), scales=scales[:, cols], in_=grp[:])
-            else:
-                bufs = {"q": 3, "k": 6, "x": 4}[key[0]]
-                ops[key] = quantized(grp[:], 512, key[0] + "c", bufs)
+        def code_tiles(width, tag, bufs):
+            codes = codes_pool.tile([P, width], U32, name="codes", tag=tag, bufs=bufs, align_bytes=64)
+            scales = codes_pool.tile([P, width], U8, name="scales", tag=tag + "_sc", bufs=bufs, align_bytes=64)
+            return codes, scales
 
-        def scores(n):
-            for g in range(2):
-                scores_half(n, g)
+        def quantise_turned(name):
+            coded[name] = codes, scales = code_tiles(512, name[0], {"q": 3, "k": 6, "x": 4}[name[0]])
+            nc.vector.quantize_mx(out=codes[:].bitcast(FP8X4), scales=scales[:], in_=ready[name][:])
 
-        def scores_half(n, g):
-            b, h, tb = n // 8, (n // 4) % 2, n % 4
-            qc, qs = ops["q", b, h]
-            cols = slice(128 * tb, 128 * tb + 128)
-            for g in (g,):
-                kc, ks = ops["k", b, h, g]
-                bank = ps_s.tile([P, 4, P], F32, name="sbank", tag="s")
-                for t in range(4):
-                    kcols = slice(128 * t, 128 * t + 128)
-                    nc.tensor.matmul_mx(
-                        out=bank[:, t, :],
-                        lhsT=kc[:, kcols].bitcast(FP8X4),
-                        lhsT_scale=ks[:, kcols],
-                        rhs=qc[:, cols].bitcast(FP8X4),
-                        rhs_scale=qs[:, cols],
-                        start=True,
-                        stop=True,
-                    )
-                ops["s", n, g] = bank
+        def quantise_v(name, half):
+            if name not in coded:
+                coded[name] = code_tiles(512, "v", 7)
+            codes, scales = coded[name]
+            cols = slice(256 * half, 256 * half + 256)
+            nc.vector.quantize_mx(out=codes[:, cols].bitcast(FP8X4), scales=scales[:, cols], in_=ready[name, half][:])
 
-        def biased(n):
-            for g in range(2):
-                biased_half(n, g)
+        def place(n):
+            return n // (H * BLOCKS), (n // BLOCKS) % H, n % BLOCKS
 
-        def biased_half(n, g):
-            h, tb = (n // 4) % 2, n % 4
-            rabt = ops["r", h, tb // 2]
-            if g == 0:
-                ops["l", n] = work.tile([P, 1024], F32, name="l", tag="l", bufs=3, align_bytes=64)
-            l = ops["l", n]
-            for g in (g,):
-                r0 = 1024 * (tb % 2) + 512 * g
-                nc.vector.scalar_tensor_tensor(
-                    out=l[:, 512 * g : 512 * g + 512].rearrange("p (m t) -> p m t", t=4),
-                    in0=ops["s", n, g][:].rearrange("p t m -> p m t"),
-                    scalar=SCALE,
-                    in1=rabt[:, r0 : r0 + 512].rearrange("p (m t) -> p m t", t=4),
-                    op0=ALU.mult,
-                    op1=ALU.add,
+        def scores(n, g):
+            b, h, blk = place(n)
+            q_codes, q_sc = coded["q%d%d" % (b, h)]
+            k_codes, k_sc = coded["k%d%d%d" % (b, h, g)]
+            rows = slice(P * blk, P * blk + P)
+            bank = score_banks.tile([P, 4, P], F32, name="score_bank", tag="score")
+            for t in range(4):
+                tokens = slice(P * t, P * t + P)
+                nc.tensor.matmul_mx(
+                    out=bank[:, t, :],
+                    lhsT=k_codes[:, tokens].bitcast(FP8X4),
+                    lhsT_scale=k_sc[:, tokens],
+                    rhs=q_codes[:, rows].bitcast(FP8X4),
+                    rhs_scale=q_sc[:, rows],
+                    start=True,
+                    stop=True,
                 )
+            live["scores", n, g] = bank
+
+        def biased(n, g):
+            h, blk = place(n)[1:]
+            if g == 0:
+                live["l", n] = work.tile([P, 2, 512], F32, name="l", tag="l", bufs=3, align_bytes=64)
+            start = 1024 * (blk % 2) + 512 * g
+            bias = ready["r%d%d" % (h, blk // 2)][:, start : start + 512]
+            nc.vector.scalar_tensor_tensor(
+                out=live["l", n][:, g, :].rearrange("p (m t) -> p m t", t=4),
+                in0=live["scores", n, g][:].rearrange("p t m -> p m t"),
+                scalar=SCALE,
+                in1=bias.rearrange("p (m t) -> p m t", t=4),
+                op0=ALU.mult,
+                op1=ALU.add,
+            )
 
         def silu(n):
-            l = ops["l", n]
-            nc.scalar.activation(out=l[:], in_=l[:], func=ACT.Silu)
+            l = live["l", n][:].rearrange("p g f -> p (g f)")
+            nc.scalar.activation(out=l, in_=l, func=ACT.Silu)
 
         def gained(n):
-            l = ops["l", n]
-            a = work.tile([P, 1024], BF16, name="a", tag="a", bufs=2, align_bytes=64)
+            a = live["a", n] = work.tile([P, 1024], BF16, name="a", tag="a", bufs=3, align_bytes=64)
             nc.vector.tensor_tensor(
                 out=a[:].rearrange("p (g m t) -> p g m t", g=2, t=4),
-                in0=l[:].rearrange("p (g m t) -> p g m t", g=2, t=4),
-                in1=c_sb[:].unsqueeze(2).to_broadcast([P, 2, P, 4]),
+                in0=live["l", n][:].rearrange("p g (m t) -> p g m t", t=4),
+                in1=gain[:].unsqueeze(2).to_broadcast([P, 2, P, 4]),
                 op=ALU.mult,
             )
-            ops["a", n] = a
 
         def quantise_a(n):
-            ops["a", n] = quantized(ops["a", n][:], 256, "ac", 12)
+            coded[n] = codes, scales = code_tiles(256, "a", 12)
+            nc.vector.quantize_mx(out=codes[:].bitcast(FP8X4), scales=scales[:], in_=live["a", n][:])
 
-        def gate(b, tb):
-            u = work.tile([P, D], F32, name="u", tag="u", bufs=5, align_bytes=64)
-            xc, xs = ops["x", b, tb // 2]
+        def gate(b, blk):
+            u = live["u", b, blk] = work.tile([P, D], F32, name="u", tag="u", bufs=5, align_bytes=64)
+            x_codes, x_sc = coded["x%d%d" % (b, blk // 2)]
             for half in range(2):
-                bank = ps_tr.tile([P, 512], F32, name="gbank", tag="tr")
-                ncols = slice(512 * half, 512 * half + 512)
+                cols = slice(512 * half, 512 * half + 512)
+                bank = turn_banks.tile([P, 512], F32, name="gate_bank", tag="turn")
                 for g in range(2):
-                    x0 = ((tb % 2) * 2 + g) * 128
+                    start = P * (2 * (blk % 2) + g)
+                    rows = slice(start, start + P)
                     nc.tensor.matmul_mx(
                         out=bank[:],
-                        lhsT=xc[:, x0 : x0 + 128].bitcast(FP8X4),
-                        lhsT_scale=xs[:, x0 : x0 + 128],
-                        rhs=wu_sb[:, g, ncols].bitcast(FP8X4),
-                        rhs_scale=wu_sc[:, g, ncols],
+                        lhsT=x_codes[:, rows].bitcast(FP8X4),
+                        lhsT_scale=x_sc[:, rows],
+                        rhs=wu_codes[:, g, cols].bitcast(FP8X4),
+                        rhs_scale=wu_sc[:, g, cols],
                         start=(g == 0),
                         stop=(g == 1),
                     )
-                nc.scalar.activation(out=u[:, ncols], in_=bank[:], func=ACT.Silu)
-            ops["u", b, tb] = u
+                nc.scalar.activation(out=u[:, cols], in_=bank[:], func=ACT.Silu)
 
-        def weighted_sum(b, tb):
-            banks = []
+        def weighted_sum(b, blk):
             for h in range(H):
-                bank = ps_o.tile([P, 512], F32, name="obank", tag="o")
-                ac, as_ = ops["a", 8 * b + 4 * h + tb]
+                bank = live["o", b, blk, h] = sum_banks.tile([P, E], F32, name="sum_bank", tag="sum")
+                a_codes, a_sc = coded[(b * H + h) * BLOCKS + blk]
                 for g in range(2):
-                    acols = slice(128 * g, 128 * g + 128)
-                    vc, vs = ops["v", b, h, g]
+                    v_codes, v_sc = coded["v%d%d%d" % (b, h, g)]
+                    rows = slice(P * g, P * g + P)
                     nc.tensor.matmul_mx(
                         out=bank[:],
-                        lhsT=ac[:, acols].bitcast(FP8X4),
-                        lhsT_scale=as_[:, acols],
-                        rhs=vc[:].bitcast(FP8X4),
-                        rhs_scale=vs[:],
+                        lhsT=a_codes[:, rows].bitcast(FP8X4),
+                        lhsT_scale=a_sc[:, rows],
+                        rhs=v_codes[:].bitcast(FP8X4),
+                        rhs_scale=v_sc[:],
                         start=(g == 0),
                         stop=(g == 1),
                     )
-                banks.append(bank)
-            ops["o", b, tb] = banks
 
-        def half_stats(b, tb):
-            stats = small.tile([P, 12], F32, name="stats", tag="stats")
+        def head_stats(b, blk):
+            stats = live["stats", b, blk] = stat.tile([P, 6 * H], F32, name="stats", tag="stats")
             for h in range(H):
-                nc.vector.bn_stats(out=stats[:, 6 * h : 6 * h + 6], in_=ops["o", b, tb][h][:])
-            ops["st", b, tb] = stats
+                nc.vector.bn_stats(out=stats[:, 6 * h : 6 * h + 6], in_=live["o", b, blk, h][:])
 
-        def row_stats(b, tb):
-            mv = small.tile([P, 2], F32, name="mv", tag="mv")
-            nc.vector.bn_aggr(out=mv[:], in_=ops["st", b, tb][:])
-            ve = small.tile([P, 1], F32, name="ve", tag="ve")
-            nc.gpsimd.tensor_scalar(out=ve[:], in0=mv[:, 1:2], scalar1=EPS, scalar2=None, op0=ALU.add)
-            rstd = small.tile([P, 1], F32, name="rstd", tag="rstd")
-            nc.gpsimd.tensor_tensor(out=rstd[:], in0=ve[:], in1=neg_half[:], op=ALU.pow)
-            ops["mv", b, tb] = mv, rstd
+        def row_stats(b, blk):
+            mean_var = live["mean_var", b, blk] = stat.tile([P, 2], F32, name="mean_var", tag="mean_var")
+            nc.vector.bn_aggr(out=mean_var[:], in_=live["stats", b, blk][:])
+            var_eps = stat.tile([P, 1], F32, name="var_eps", tag="var_eps")
+            nc.gpsimd.tensor_scalar(out=var_eps[:], in0=mean_var[:, 1:2], scalar1=EPS, scalar2=None, op0=ALU.add)
+            rstd = live["rstd", b, blk] = stat.tile([P, 1], F32, name="rstd", tag="rstd")
+            nc.gpsimd.tensor_tensor(out=rstd[:], in0=var_eps[:], in1=neg_half[:], op=ALU.pow)
 
-        def gated(b, tb):
-            u, mv = ops["u", b, tb], ops["mv", b, tb][0]
-            y = work.tile([P, D], F32, name="y", tag="y", bufs=3, align_bytes=64)
+        def gated(b, blk):
+            y = live["y", b, blk] = work.tile([P, D], F32, name="y", tag="y", bufs=3, align_bytes=64)
             for h in range(H):
-                hc = slice(512 * h, 512 * h + 512)
+                cols = slice(E * h, E * h + E)
                 nc.vector.scalar_tensor_tensor(
-                    out=y[:, hc],
-                    in0=ops["o", b, tb][h][:],
-                    scalar=mv[:, 0:1],
-                    in1=u[:, hc],
+                    out=y[:, cols],
+                    in0=live["o", b, blk, h][:],
+                    scalar=live["mean_var", b, blk][:, 0:1],
+                    in1=live["u", b, blk][:, cols],
                     op0=ALU.subtract,
                     op1=ALU.mult,
                 )
-            ops["y", b, tb] = y
 
-        def scaled(b, tb):
-            y, rstd = ops["y", b, tb], ops["mv", b, tb][1]
-            yb = work.tile([P, 2, 512], BF16, name="yb", tag="yb", bufs=2, align_bytes=64)
+        def scaled(b, blk):
+            y, rstd = live["y", b, blk], live["rstd", b, blk]
+            y_bf = live["y_bf", b, blk] = work.tile([P, H, E], BF16, name="y_bf", tag="y_bf", bufs=2, align_bytes=64)
             for h in range(H):
-                nc.scalar.activation(out=yb[:, h, :], in_=y[:, 512 * h : 512 * h + 512], func=ACT.Copy, scale=rstd[:])
+                nc.scalar.activation(out=y_bf[:, h, :], in_=y[:, E * h : E * h + E], func=ACT.Copy, scale=rstd[:])
             nc.scalar.activation(out=y[:], in_=y[:], func=ACT.Copy, scale=rstd[:])
-            nc.sync.dma_start(out=out_0[b, 128 * tb : 128 * tb + 128, :], in_=y[:])
-            ops["yb", b, tb] = yb
 
-        def turned_result(b, tb):
-            ygrp = work.tile([P, 1024], BF16, name="ygrp", tag="ygrp", bufs=2, align_bytes=64)
-            turn(words_of(ops["yb", b, tb]), ygrp[:].bitcast(F32).rearrange("p (a m u) -> p a m u", a=2, u=2), "S")
-            ops["yg", b, tb] = ygrp
+        def store_result(b, blk):
+            nc.sync.dma_start(out=out_0[b, P * blk : P * blk + P, :], in_=live["y", b, blk][:])
 
-        def planes(b, tb):
-            oc, os_ = quantized(ops["yg", b, tb][:], 256, "oc", 3)
-            m0 = 512 * b + 128 * tb
+        def turned_result(b, blk):
+            tile = live["y_turned", b, blk] = work.tile([P, 1024], BF16, name="y_turned", tag="y_turned", bufs=2, align_bytes=64)
+            dst = tile[:].bitcast(F32).rearrange("p (a m e) -> p a m e", a=2, e=2)
+            turn(as_words(live["y_bf", b, blk]), dst, "S")
+
+        def planes(b, blk):
+            codes, scales = code_tiles(256, "y", 3)
+            nc.vector.quantize_mx(out=codes[:].bitcast(FP8X4), scales=scales[:], in_=live["y_turned", b, blk][:])
+            first = T * b + P * blk
+            words = out_1.rearrange("g p m t -> g p (m t)").bitcast(I32).rearrange("g p m -> p g m")
             nc.sync.dma_start(
-                out=out_1.rearrange("g p m t -> g p (m t)").bitcast(I32)[:, :, m0 : m0 + 128].rearrange("g p m -> p g m"),
-                in_=oc[:].bitcast(I32).rearrange("p (g m) -> p g m", g=2),
+                out=words[:, :, first : first + P],
+                in_=codes[:].bitcast(I32).rearrange("p (g m) -> p g m", g=2),
             )
-            for quad in range(4):
+            rows = out_2.bitcast(I32).rearrange("g r m -> r g m")
+            for j in range(4):
                 nc.sync.dma_start(
-                    out=out_2.bitcast(I32)[:, 4 * quad : 4 * quad + 4, m0 // 4 : m0 // 4 + 32].rearrange("g r m -> r g m"),
-                    in_=os_[32 * quad : 32 * quad + 4].bitcast(I32).rearrange("r (g m) -> r g m", g=2),
+                    out=rows[4 * j : 4 * j + 4, :, first // 4 : first // 4 + P // 4],
+                    in_=scales[32 * j : 32 * j + 4].bitcast(I32).rearrange("r (g m) -> r g m", g=2),
                 )
 
-        def run(word):
-            kind = word[0]
-            if kind in "qkxr":
-                name, engines = word.split("/") if "/" in word else (word, "SS")
-                key = [int(ch) for ch in name[1:]]
-                if kind == "r":
-                    prep_rab(*key, engines=engines)
-                else:
-                    prep(kind, *key, engines=engines)
-            elif kind == "v":
-                name, engine = word.split("/") if "/" in word else (word, "G")
-                prep_v(*[int(ch) for ch in name[1:]], engine=engine)
-            elif kind == "Q":
-                quantise((word[1],) + tuple(int(ch) for ch in word[2:]))
-            elif kind in "se":
-                n, g = [int(num) for num in word[2:].split(",")]
-                (scores_half if kind == "s" else biased_half)(n, g)
+        def prepare(item):
+            name, engine = (item.split("/") + [""])[:2]
+            if name[0] == "g":
+                gate(int(name[1]), int(name[2]))
+            elif name[0] == "v":
+                interleave(name[:4], int(name[5]), engine or "G")
             else:
-                name, key = word.split(":")
-                key = [int(n) for n in key.split(",")]
-                table = {
-                    "S": scores, "E": biased, "F": silu, "G": gained, "D": quantise_a, "g": gate,
-                    "O": weighted_sum, "B": half_stats, "A": row_stats, "Y": gated, "Z": scaled, "T": turned_result, "P": planes,
-                }
-                table[name](*key)
+                turn_input(name, engine or "SS")
+
+        def prepared_in(n):
+            early, late = PLAN.get(n, ("", ""))
+            return [item.split("/")[0] for item in (early + " " + late).split()]
+
+        def step(n):
+            early, late = PLAN.get(n, ("", ""))
+            summed, turned, leaving = finish.get(n), finish.get(n - 1), finish.get(n - 2)
+            if n + 1 < UNITS:
+                biased(n + 1, 0)
+            if summed:
+                weighted_sum(*summed)
+                head_stats(*summed)
+            if n + 1 < UNITS:
+                biased(n + 1, 1)
+            if turned:
+                scaled(*turned)
+            if summed:
+                row_stats(*summed)
+            if 0 <= n - 1 < UNITS:
+                quantise_a(n - 1)
+            for name in prepared_in(n - 1):
+                if name[0] in "qkx":
+                    quantise_turned(name)
+            for item in early.split():
+                prepare(item)
+            if n + 1 < UNITS:
+                silu(n + 1)
+            if summed:
+                gated(*summed)
+            if n < UNITS:
+                gained(n)
+            for name in prepared_in(n - 1):
+                if name[0] == "v":
+                    quantise_v(name[:4], int(name[5]))
+            for item in late.split():
+                prepare(item)
+            if n + 2 < UNITS:
+                scores(n + 2, 0)
+                scores(n + 2, 1)
+            if turned:
+                turned_result(*turned)
+            if leaving:
+                planes(*leaving)
+            if turned:
+                store_result(*turned)
+
+        finish = {FIRST_FINISH[b] + blk: (b, blk) for b in range(B) for blk in range(BLOCKS)}
 
         with tc.manual_schedule():
-            for word in PROGRAM.split():
-                run(word)
+            for name in LOADS.split():
+                load(name)
+            turn_input("q00", "SV")
+            quantise_turned("q00")
+            turn_input("k000", "SV")
+            quantise_turned("k000")
+            turn_input("k001", "SV")
+            turn_input("r00", "SS")
+            quantise_turned("k001")
+            scores(0, 0)
+            scores(0, 1)
+            biased(0, 0)
+            biased(0, 1)
+            scores(1, 0)
+            scores(1, 1)
+            silu(0)
+            for n in range(STEPS):
+                step(n)

from contextlib import ExitStack

import concourse.mybir as mybir
from concourse.masks import make_identity

B, H, T, S, E = 2, 2, 512, 1024, 512
D = H * E
EPS = 1e-5
SCALE = 1.0 / float(E) ** 0.5
FLOPS = 2 * (2 * B * H * T * S * E + B * T * D * D)

F32 = mybir.dt.float32
BF16 = mybir.dt.bfloat16
U32 = mybir.dt.uint32
I32 = mybir.dt.int32
U8 = mybir.dt.uint8
FP8X4 = mybir.dt.float8_e4m3fn_x4
ALU = mybir.AluOpType
ACT = mybir.ActivationFunctionType

P = 128
GROUP = 512
BLOCKS = T // P
UNITS = B * H * BLOCKS

LOADS = (
    "q00 k000 k001 r00 r01 k010 v000 k011 q01 v011 v010 v001 r10 r11 x00 v101 x01 "
    "q10 k101 k100 k110 wu k111 x11 q11 x10 v100 v110 v111"
)

PLAN = {
    0: ("k010/SV", "r01 v000.1 v000.0/S"),
    1: ("k011", "q01 v001.1 v010.0/S"),
    2: ("r10", "v010.1/S"),
    3: ("x00", "v001.0"),
    4: ("r11", "x01/SV"),
    5: ("q10", "k101 k100 v011.1 v011.0/S"),
    6: ("g01", ""),
    7: ("g00", "g03 v100.0"),
    8: ("k111", "q11 v110.0/S v100.1"),
    9: ("g02", "k110 v110.1/S v101.0"),
    10: ("x11", "v111.1/S v101.1"),
    11: ("x10", ""),
    12: ("", "v111.0/S"),
    13: ("g11", ""),
    14: ("g10", ""),
    15: ("g13", "g12"),
}
STEPS = 20
FIRST_FINISH = (8, 14)


def tile_hstupointwisetransducer_x2_kernel(
    tc, q, k, rab, c, v, x, wu_words, wu_scales, out_0, out_1, out_2
):
    nc = tc.nc
    with ExitStack() as ctx:
        const = ctx.enter_context(tc.tile_pool(name="const", bufs=1))
        inputs = ctx.enter_context(tc.tile_pool(name="inputs", bufs=9))
        ordered = ctx.enter_context(tc.tile_pool(name="ordered", bufs=5))
        codes_pool = ctx.enter_context(tc.tile_pool(name="codes_pool", bufs=1))
        work = ctx.enter_context(tc.tile_pool(name="work", bufs=3))
        stat = ctx.enter_context(tc.tile_pool(name="stat", bufs=4))
        turn_banks = ctx.enter_context(tc.psum_pool(name="turn_banks", bufs=4))
        score_banks = ctx.enter_context(tc.psum_pool(name="score_banks", bufs=2))
        sum_banks = ctx.enter_context(tc.psum_pool(name="sum_banks", bufs=2))

        ident = const.tile([P, P], F32, name="ident")
        make_identity(nc, ident[:])
        neg_half = const.tile([P, 1], F32, name="neg_half")
        nc.gpsimd.memset(neg_half[:], -0.5)
        wu_sc = const.tile([P, 2, D], U8, name="wu_sc", align_bytes=64)
        nc.gpsimd.memset(wu_sc[:].rearrange("p g n -> p (g n)").bitcast(U32), 0)
        wu_codes = const.tile([P, 2, D], U32, name="wu_codes", align_bytes=64)
        gain = const.tile([P, 2, 4], BF16, name="gain")
        nc.scalar.dma_start(out=gain[:], in_=c.rearrange("(g p t) -> p g t", g=2, t=4))

        raw = {}
        ready = {}
        coded = {}
        live = {}

        def load(name):
            if name == "wu":
                nc.sync.dma_start(
                    out=wu_codes[:].bitcast(I32),
                    in_=wu_words.rearrange("g p n t -> g p (n t)").bitcast(I32).rearrange("g p n -> p g n"),
                )
                for j in range(4):
                    nc.sync.dma_start(
                        out=wu_sc[32 * j : 32 * j + 4].bitcast(I32),
                        in_=wu_scales.bitcast(I32)[:, 4 * j : 4 * j + 4].rearrange("g r n -> r g n"),
                    )
                return
            kind, key = name[0], [int(digit) for digit in name[1:]]
            if kind == "v":
                raw[name] = inputs.tile([P, 4, 512], BF16, name=name, tag="v_raw", bufs=4, align_bytes=64)
            else:
                raw[name] = inputs.tile([P, 4, 512], BF16, name=name, tag="raw", align_bytes=64)
            dst = raw[name][:]
            if kind == "q":
                src = q[key[0], key[1]].rearrange("(a r) e -> r a e", r=P)
            elif kind in "kv":
                tensor = k if kind == "k" else v
                rows = slice(GROUP * key[2], GROUP * key[2] + GROUP)
                src = tensor[key[0], key[1], rows].rearrange("(r t) e -> r t e", t=4)
            else:
                tensor = rab if kind == "r" else x
                src = tensor[key[0], 256 * key[1] : 256 * key[1] + 256].rearrange("(a r) s -> r a s", r=P)
                dst = dst.rearrange("p (a g) e -> p a (g e)", g=2)
            nc.sync.dma_start(out=dst, in_=src)

        def copy(engine, out, in_):
            if engine == "V":
                nc.vector.tensor_copy(out=out, in_=in_)
            else:
                nc.scalar.copy(out=out, in_=in_)

        def as_words(tile):
            flat = tile[:].rearrange("p a e -> p (a e)").bitcast(F32)
            return flat.rearrange("p (a w) -> p a w", w=256)

        def turn(words, dst, engine):
            bank = turn_banks.tile([P, 2, 2, P], F32, name="turn_bank", tag="turn")
            for a in range(2):
                for e in range(2):
                    nc.tensor.transpose(bank[:, a, e, :], words[:, a, e::2], ident[:])
            copy(engine, dst, bank[:].rearrange("p a e m -> p a m e"))

        def turn_input(name, engines):
            tag, bufs = ("rab_turned", 4) if name[0] == "r" else ("ordered", 5)
            tile = ordered.tile([P, 2048], BF16, name="turned", tag=tag, bufs=bufs, align_bytes=64)
            dst = tile[:].bitcast(F32).rearrange("p (a m e) -> p a m e", a=4, e=2)
            for i in range(2):
                runs = slice(2 * i, 2 * i + 2)
                turn(as_words(raw[name])[:, runs], dst[:, runs], engines[i])
            ready[name] = tile

        def interleave(name, half, engine):
            tile = ordered.tile([P, 1024], BF16, name="mixed", tag="mixed_" + engine, bufs=1, align_bytes=64)
            out = tile[:].rearrange("p (e t) -> p e t", t=4)
            in_ = raw[name][:, :, 256 * half : 256 * half + 256].rearrange("p t e -> p e t")
            if engine == "G":
                nc.gpsimd.tensor_scalar(out=out, in0=in_, scalar1=1.0, scalar2=0.0, op0=ALU.mult, op1=ALU.add)
            else:
                copy(engine, out, in_)
            ready[name, half] = tile

        def code_tiles(width, tag, bufs):
            codes = codes_pool.tile([P, width], U32, name="codes", tag=tag, bufs=bufs, align_bytes=64)
            scales = codes_pool.tile([P, width], U8, name="scales", tag=tag + "_sc", bufs=bufs, align_bytes=64)
            return codes, scales

        def quantise_turned(name):
            coded[name] = codes, scales = code_tiles(512, name[0], {"q": 3, "k": 6, "x": 4}[name[0]])
            nc.vector.quantize_mx(out=codes[:].bitcast(FP8X4), scales=scales[:], in_=ready[name][:])

        def quantise_v(name, half):
            if name not in coded:
                coded[name] = code_tiles(512, "v", 7)
            codes, scales = coded[name]
            cols = slice(256 * half, 256 * half + 256)
            nc.vector.quantize_mx(out=codes[:, cols].bitcast(FP8X4), scales=scales[:, cols], in_=ready[name, half][:])

        def place(n):
            return n // (H * BLOCKS), (n // BLOCKS) % H, n % BLOCKS

        def scores(n, g):
            b, h, blk = place(n)
            q_codes, q_sc = coded["q%d%d" % (b, h)]
            k_codes, k_sc = coded["k%d%d%d" % (b, h, g)]
            rows = slice(P * blk, P * blk + P)
            bank = score_banks.tile([P, 4, P], F32, name="score_bank", tag="score")
            for t in range(4):
                tokens = slice(P * t, P * t + P)
                nc.tensor.matmul_mx(
                    out=bank[:, t, :],
                    lhsT=k_codes[:, tokens].bitcast(FP8X4),
                    lhsT_scale=k_sc[:, tokens],
                    rhs=q_codes[:, rows].bitcast(FP8X4),
                    rhs_scale=q_sc[:, rows],
                    start=True,
                    stop=True,
                )
            live["scores", n, g] = bank

        def biased(n, g):
            h, blk = place(n)[1:]
            if g == 0:
                live["l", n] = work.tile([P, 2, 512], F32, name="l", tag="l", bufs=3, align_bytes=64)
            start = 1024 * (blk % 2) + 512 * g
            bias = ready["r%d%d" % (h, blk // 2)][:, start : start + 512]
            nc.vector.scalar_tensor_tensor(
                out=live["l", n][:, g, :].rearrange("p (m t) -> p m t", t=4),
                in0=live["scores", n, g][:].rearrange("p t m -> p m t"),
                scalar=SCALE,
                in1=bias.rearrange("p (m t) -> p m t", t=4),
                op0=ALU.mult,
                op1=ALU.add,
            )

        def silu(n):
            l = live["l", n][:].rearrange("p g f -> p (g f)")
            nc.scalar.activation(out=l, in_=l, func=ACT.Silu)

        def gained(n):
            a = live["a", n] = work.tile([P, 1024], BF16, name="a", tag="a", bufs=3, align_bytes=64)
            nc.vector.tensor_tensor(
                out=a[:].rearrange("p (g m t) -> p g m t", g=2, t=4),
                in0=live["l", n][:].rearrange("p g (m t) -> p g m t", t=4),
                in1=gain[:].unsqueeze(2).to_broadcast([P, 2, P, 4]),
                op=ALU.mult,
            )

        def quantise_a(n):
            coded[n] = codes, scales = code_tiles(256, "a", 12)
            nc.vector.quantize_mx(out=codes[:].bitcast(FP8X4), scales=scales[:], in_=live["a", n][:])

        def gate(b, blk):
            u = live["u", b, blk] = work.tile([P, D], F32, name="u", tag="u", bufs=5, align_bytes=64)
            x_codes, x_sc = coded["x%d%d" % (b, blk // 2)]
            for half in range(2):
                cols = slice(512 * half, 512 * half + 512)
                bank = turn_banks.tile([P, 512], F32, name="gate_bank", tag="turn")
                for g in range(2):
                    start = P * (2 * (blk % 2) + g)
                    rows = slice(start, start + P)
                    nc.tensor.matmul_mx(
                        out=bank[:],
                        lhsT=x_codes[:, rows].bitcast(FP8X4),
                        lhsT_scale=x_sc[:, rows],
                        rhs=wu_codes[:, g, cols].bitcast(FP8X4),
                        rhs_scale=wu_sc[:, g, cols],
                        start=(g == 0),
                        stop=(g == 1),
                    )
                nc.scalar.activation(out=u[:, cols], in_=bank[:], func=ACT.Silu)

        def weighted_sum(b, blk):
            for h in range(H):
                bank = live["o", b, blk, h] = sum_banks.tile([P, E], F32, name="sum_bank", tag="sum")
                a_codes, a_sc = coded[(b * H + h) * BLOCKS + blk]
                for g in range(2):
                    v_codes, v_sc = coded["v%d%d%d" % (b, h, g)]
                    rows = slice(P * g, P * g + P)
                    nc.tensor.matmul_mx(
                        out=bank[:],
                        lhsT=a_codes[:, rows].bitcast(FP8X4),
                        lhsT_scale=a_sc[:, rows],
                        rhs=v_codes[:].bitcast(FP8X4),
                        rhs_scale=v_sc[:],
                        start=(g == 0),
                        stop=(g == 1),
                    )

        def head_stats(b, blk):
            stats = live["stats", b, blk] = stat.tile([P, 6 * H], F32, name="stats", tag="stats")
            for h in range(H):
                nc.vector.bn_stats(out=stats[:, 6 * h : 6 * h + 6], in_=live["o", b, blk, h][:])

        def row_stats(b, blk):
            mean_var = live["mean_var", b, blk] = stat.tile([P, 2], F32, name="mean_var", tag="mean_var")
            nc.vector.bn_aggr(out=mean_var[:], in_=live["stats", b, blk][:])
            var_eps = stat.tile([P, 1], F32, name="var_eps", tag="var_eps")
            nc.gpsimd.tensor_scalar(out=var_eps[:], in0=mean_var[:, 1:2], scalar1=EPS, scalar2=None, op0=ALU.add)
            rstd = live["rstd", b, blk] = stat.tile([P, 1], F32, name="rstd", tag="rstd")
            nc.gpsimd.tensor_tensor(out=rstd[:], in0=var_eps[:], in1=neg_half[:], op=ALU.pow)

        def gated(b, blk):
            y = live["y", b, blk] = work.tile([P, D], F32, name="y", tag="y", bufs=3, align_bytes=64)
            for h in range(H):
                cols = slice(E * h, E * h + E)
                nc.vector.scalar_tensor_tensor(
                    out=y[:, cols],
                    in0=live["o", b, blk, h][:],
                    scalar=live["mean_var", b, blk][:, 0:1],
                    in1=live["u", b, blk][:, cols],
                    op0=ALU.subtract,
                    op1=ALU.mult,
                )

        def scaled(b, blk):
            y, rstd = live["y", b, blk], live["rstd", b, blk]
            y_bf = live["y_bf", b, blk] = work.tile([P, H, E], BF16, name="y_bf", tag="y_bf", bufs=2, align_bytes=64)
            for h in range(H):
                nc.scalar.activation(out=y_bf[:, h, :], in_=y[:, E * h : E * h + E], func=ACT.Copy, scale=rstd[:])
            nc.scalar.activation(out=y[:], in_=y[:], func=ACT.Copy, scale=rstd[:])

        def store_result(b, blk):
            nc.sync.dma_start(out=out_0[b, P * blk : P * blk + P, :], in_=live["y", b, blk][:])

        def turned_result(b, blk):
            tile = live["y_turned", b, blk] = work.tile([P, 1024], BF16, name="y_turned", tag="y_turned", bufs=2, align_bytes=64)
            dst = tile[:].bitcast(F32).rearrange("p (a m e) -> p a m e", a=2, e=2)
            turn(as_words(live["y_bf", b, blk]), dst, "S")

        def planes(b, blk):
            codes, scales = code_tiles(256, "y", 3)
            nc.vector.quantize_mx(out=codes[:].bitcast(FP8X4), scales=scales[:], in_=live["y_turned", b, blk][:])
            first = T * b + P * blk
            words = out_1.rearrange("g p m t -> g p (m t)").bitcast(I32).rearrange("g p m -> p g m")
            nc.sync.dma_start(
                out=words[:, :, first : first + P],
                in_=codes[:].bitcast(I32).rearrange("p (g m) -> p g m", g=2),
            )
            rows = out_2.bitcast(I32).rearrange("g r m -> r g m")
            for j in range(4):
                nc.sync.dma_start(
                    out=rows[4 * j : 4 * j + 4, :, first // 4 : first // 4 + P // 4],
                    in_=scales[32 * j : 32 * j + 4].bitcast(I32).rearrange("r (g m) -> r g m", g=2),
                )

        def prepare(item):
            name, engine = (item.split("/") + [""])[:2]
            if name[0] == "g":
                gate(int(name[1]), int(name[2]))
            elif name[0] == "v":
                interleave(name[:4], int(name[5]), engine or "G")
            else:
                turn_input(name, engine or "SS")

        def prepared_in(n):
            early, late = PLAN.get(n, ("", ""))
            return [item.split("/")[0] for item in (early + " " + late).split()]

        def step(n):
            early, late = PLAN.get(n, ("", ""))
            summed, turned, leaving = finish.get(n), finish.get(n - 1), finish.get(n - 2)
            if n + 1 < UNITS:
                biased(n + 1, 0)
            if summed:
                weighted_sum(*summed)
                head_stats(*summed)
            if n + 1 < UNITS:
                biased(n + 1, 1)
            if turned:
                scaled(*turned)
            if summed:
                row_stats(*summed)
            if 0 <= n - 1 < UNITS:
                quantise_a(n - 1)
            for name in prepared_in(n - 1):
                if name[0] in "qkx":
                    quantise_turned(name)
            for item in early.split():
                prepare(item)
            if n + 1 < UNITS:
                silu(n + 1)
            if summed:
                gated(*summed)
            if n < UNITS:
                gained(n)
            for name in prepared_in(n - 1):
                if name[0] == "v":
                    quantise_v(name[:4], int(name[5]))
            for item in late.split():
                prepare(item)
            if n + 2 < UNITS:
                scores(n + 2, 0)
                scores(n + 2, 1)
            if turned:
                turned_result(*turned)
            if leaving:
                planes(*leaving)
            if turned:
                store_result(*turned)

        finish = {FIRST_FINISH[b] + blk: (b, blk) for b in range(B) for blk in range(BLOCKS)}

        with tc.manual_schedule():
            for name in LOADS.split():
                load(name)
            turn_input("q00", "SV")
            quantise_turned("q00")
            turn_input("k000", "SV")
            quantise_turned("k000")
            turn_input("k001", "SV")
            turn_input("r00", "SS")
            quantise_turned("k001")
            scores(0, 0)
            scores(0, 1)
            biased(0, 0)
            biased(0, 1)
            scores(1, 0)
            scores(1, 1)
            silu(0)
            for n in range(STEPS):
                step(n)
